import numpy as np
import ml_dtypes


def mxq(x, axis, fmt="e4m3"):
    dtype, down = {"e4m3": (ml_dtypes.float8_e4m3fn, 7), "e5m2": (ml_dtypes.float8_e5m2, 14)}[fmt]
    v = np.moveaxis(np.asarray(x, np.float32).astype(ml_dtypes.bfloat16).astype(np.float64), axis, -1)
    blocks = v.reshape(v.shape[:-1] + (-1, 32))
    amax = np.abs(blocks).max(-1, keepdims=True)
    byte = np.maximum(np.where(amax > 0, np.frexp(amax)[1] - 1 + 127, 0) - down, 1)
    scale = np.exp2(byte - 127.0)
    codes = (blocks / scale).astype(np.float32).astype(dtype).astype(np.float64)
    return np.moveaxis((codes * scale).reshape(v.shape), -1, axis)


WIDE = False


def mx_kscale(k):
    if not WIDE:
        return np.ones(k)
    levels = np.array([10, -10, 5, -5, 0])
    if k % 512:
        return np.exp2(np.random.permutation(np.resize(levels, k // 32))).repeat(32)
    a = np.empty((k // 512, 16))
    for p in range(k // 512):
        a[p, :8] = np.random.permutation(np.resize(levels, 8))
        for g in range(8):
            far = levels[np.abs(levels - a[p, g]) >= 10]
            a[p, g + 8] = far[np.random.randint(len(far))]
    return np.exp2(a.ravel()).repeat(32)


def f64(x):
    return np.asarray(x).astype(np.float64)


def striped(idx):
    return np.tile(idx.reshape(-1, 16).T, (8, 1)).astype(np.uint16)


def unstriped(offs):
    return offs[:16].T.reshape(-1).astype(np.int64)


def striped8(idx):
    return np.concatenate([x.reshape(-1, 16).T for x in idx]).astype(np.uint16)


def runs(offs, k):
    lists = np.stack([offs[16 * r : 16 * r + 16].T.reshape(-1) for r in range(8)]).astype(np.int64)
    return lists[np.arange(k) % 512 // 64]


def pack_weight(w):
    k, n = w.shape
    w = f64(np.asarray(w, np.float32).astype(ml_dtypes.bfloat16)).reshape(k // 32, 32, n)
    amax = np.abs(w).max(1)
    byte = np.clip(np.where(amax > 0, np.frexp(amax)[1] - 1 + 127 - 7, 1), 1, 254)
    scaled = (w * np.exp2(127.0 - byte)[:, None, :]).reshape(k, n).astype(np.float32)
    words = np.ascontiguousarray(scaled.reshape(k // 512, 128, 4, n).transpose(0, 1, 3, 2)).astype(ml_dtypes.float8_e4m3fn).view(np.uint8)
    return words, np.ascontiguousarray(byte.astype(np.uint8).reshape(k // 512, 16, n))


def unpack_weight(words, scales):
    g, p, n, _ = words.shape
    vals = np.ascontiguousarray(words).view(ml_dtypes.float8_e4m3fn).astype(np.float64) * np.repeat(np.exp2(scales.astype(np.float64) - 127.0), 8, axis=1)[..., None]
    return vals.transpose(0, 1, 3, 2).reshape(g * 512, n)


def sigmoid(v):
    return 1.0 / (1.0 + np.exp(-np.maximum(v, -700.0)))


K, T, S, N, H = 512, 2048, 512, 512, 512


def setup_inputs():
    n = np.random.standard_normal
    s = mx_kscale(K)[:, None]
    u = mx_kscale(S)
    packed_xT = pack_weight(n((K, T)) * s)
    return {
        "x_words": packed_xT[0],
        "x_scales": packed_xT[1],
        "wa": (n((K, H)) / np.sqrt(K) / s).astype(np.float32),
        "gt": (np.random.uniform(0.5, 1.5, (S, 1)) * u[:, None]).astype(np.float32),
        "w1": (n((S, N)) / np.sqrt(S) / u[:, None]).astype(np.float32),
        "offs": striped(np.random.permutation(T)[:S]),
        "n1": striped8(np.stack([np.random.permutation(H) for _ in range(8)])),
        "n2": striped8(np.stack([np.random.permutation(H) for _ in range(8)])),
        "n3": striped8(np.stack([np.random.permutation(H) for _ in range(8)])),
        "n4": striped8(np.stack([np.random.permutation(H) for _ in range(8)])),
    }


def reference(x_words, x_scales, wa, gt, w1, offs, n1, n2, n3, n4):
    xq = unpack_weight(x_words, x_scales)[:, unstriped(offs)]
    y = xq.T @ mxq(f64(wa), 0, "e4m3")
    z = f64(gt) * (np.minimum(np.maximum(y, y[np.arange(S)[:, None], runs(n1, S)]), y[np.arange(S)[:, None], runs(n2, S)]))
    h = mxq(f64(w1), 0, "e4m3").T @ mxq(z, 0, "e4m3")
    return h + (sigmoid(h[np.arange(N)[:, None], runs(n3, N)])) * (h[np.arange(N)[:, None], runs(n4, N)] - h)

@@ -1,0 +1,247 @@
+from contextlib import ExitStack
+
+import concourse.mybir as mybir
+
+FLOPS = 2 * 2 * 512 * 512 * 512
+
+F32 = mybir.dt.float32
+BF16 = mybir.dt.bfloat16
+I32 = mybir.dt.int32
+U32 = mybir.dt.uint32
+U16 = mybir.dt.uint16
+U8 = mybir.dt.uint8
+FP8X4 = mybir.dt.float8_e4m3fn_x4
+ALU = mybir.AluOpType
+ACT = mybir.ActivationFunctionType
+
+P = 128
+PACK = 4
+T = 2048
+W = 512
+HALF = 256
+Z_CHUNKS = ((0, 256), (256, 384), (384, 512))
+
+
+def tile_picked_tokminmxtrack_none_p_kernel(tc, x_words, x_scales, wa, gt, w1, offs, n1, n2, n3, n4, out):
+    nc = tc.nc
+    with ExitStack() as ctx:
+        lists = ctx.enter_context(tc.tile_pool(name="lists", bufs=1))
+        sb = ctx.enter_context(tc.tile_pool(name="sb", bufs=1))
+        ps = ctx.enter_context(tc.psum_pool(name="ps", bufs=1))
+
+        def load_list(src, name):
+            tile = lists.tile([P, W // 16], U16, name=name)
+            nc.sync.dma_start(tile[:], src)
+            return tile
+
+        def entries(tile, c0, c1):
+            return tile[:, c0 // 16 : c1 // 16]
+
+        def interleave(engine_copy, dst, src):
+            engine_copy(
+                dst.rearrange("p (c i) t -> p c t i", i=4),
+                src.rearrange("p t (c i) -> p c t i", i=4),
+            )
+
+        def quantize(codes, scales, grouped):
+            nc.vector.quantize_mx(out=codes.bitcast(FP8X4), scales=scales, in_=grouped.rearrange("p c t -> p (c t)"))
+
+        def product(acc, l_codes, l_scales, r_codes, r_scales):
+            nc.tensor.matmul_mx(
+                out=acc, lhsT=l_codes.bitcast(FP8X4), lhsT_scale=l_scales,
+                rhs=r_codes.bitcast(FP8X4), rhs_scale=r_scales, start=True, stop=True,
+            )
+
+        x_bytes = sb.tile([P, T], U8, name="x_bytes", align_bytes=64)
+        nc.vector.memset(x_bytes[:].bitcast(I32), 0)
+        warm = sb.tile([P, 8], F32, name="warm")
+        nc.gpsimd.memset(warm[:], 0.0)
+        nc.scalar.activation(warm[:, 4:8], warm[:, 0:4], ACT.Sigmoid)
+        y_win = [sb.tile([P, 2 * W if t < 3 else W], F32, name="y_win%d" % t) for t in range(PACK)]
+        for t in range(3):
+            nc.vector.memset(y_win[t][:, W:], 0.0)
+
+        offs_t = load_list(offs, "offs_t")
+        gt_t = sb.tile([P, PACK], F32, name="gt_t")
+        nc.sync.dma_start(gt_t[:], gt.rearrange("(p t) o -> p (t o)", t=PACK))
+        for q in range(4):
+            nc.scalar.dma_start(
+                x_bytes[32 * q : 32 * q + 4, :].bitcast(I32), x_scales[0, 4 * q : 4 * q + 4, :].bitcast(I32)
+            )
+        wa_rows = wa.rearrange("(p j) n -> p j n", j=PACK)
+        wa_raw = []
+        for u in range(2):
+            raw = sb.tile([P, PACK, HALF], F32, name="wa_raw%d" % u)
+            nc.sync.dma_start(raw[:], wa_rows[:, :, u * HALF : (u + 1) * HALF])
+            wa_raw.append(raw)
+        x_codes = sb.tile([P, T], U32, name="x_codes", align_bytes=64)
+        nc.sync.dma_start(x_codes[:].bitcast(I32), x_words[0].rearrange("p n t -> p (n t)").bitcast(I32))
+        n1_t = load_list(n1, "n1_t")
+        n2_t = load_list(n2, "n2_t")
+        w1_raw = sb.tile([P, PACK, W], F32, name="w1_raw")
+        nc.sync.dma_start(w1_raw[:], w1.rearrange("(p j) n -> p j n", j=PACK))
+        n3_t = load_list(n3, "n3_t")
+        n4_t = load_list(n4, "n4_t")
+
+        gt_pos = sb.tile([P, PACK], F32, name="gt_pos")
+        nc.gpsimd.tensor_scalar(gt_pos[:], gt_t[:], 0.0, 2.0, ALU.is_ge, ALU.mult)
+        gt_sign = sb.tile([P, PACK], F32, name="gt_sign")
+        nc.gpsimd.tensor_scalar(gt_sign[:], gt_pos[:], 1.0, -1.0, ALU.mult, ALU.add)
+        gt_abs = sb.tile([P, PACK], F32, name="gt_abs")
+        nc.gpsimd.tensor_tensor(gt_abs[:], gt_t[:], gt_sign[:], ALU.mult)
+
+        picked_bytes = sb.tile([P, W], U8, name="picked_bytes", align_bytes=64)
+        nc.vector.tensor_copy(picked_bytes[:], x_bytes[:].indirect(offs_t[:]))
+        tok_scales = sb.tile([P, W], U8, name="tok_scales", align_bytes=64)
+        nc.vector.tensor_copy(
+            tok_scales[:].rearrange("p (t m) -> p t m", t=PACK), picked_bytes[:].rearrange("p (m t) -> p t m", t=PACK)
+        )
+
+        wa_codes = sb.tile([P, W], U32, name="wa_codes", align_bytes=64)
+        wa_scales = sb.tile([P, W], U8, name="wa_scales", align_bytes=64)
+        for u in range(2):
+            grouped = sb.tile([P, HALF, PACK], BF16, name="wa_grouped%d" % u, align_bytes=64)
+            interleave(nc.scalar.copy, grouped[:], wa_raw[u][:])
+            quantize(wa_codes[:, u * HALF : (u + 1) * HALF], wa_scales[:, u * HALF : (u + 1) * HALF], grouped[:])
+
+        tok_codes = sb.tile([P, W], U32, name="tok_codes", align_bytes=64)
+        nc.vector.tensor_copy(tok_codes[:].rearrange("p (t m) -> p m t", t=PACK), x_codes[:].indirect(offs_t[:]))
+
+        y_bf = sb.tile([P, PACK, W], BF16, name="y_bf", align_bytes=64)
+        for t in range(PACK):
+            l_codes = tok_codes[:, t * P : (t + 1) * P]
+            l_scales = tok_scales[:, t * P : (t + 1) * P]
+            if t == 0:
+                acc_a = ps.tile([P, W], F32, name="acc_a", tag="bank0")
+                acc_b = ps.tile([P, W], F32, name="acc_b", tag="bank4")
+                product(acc_a[:, :HALF], l_codes, l_scales, wa_codes[:, :HALF], wa_scales[:, :HALF])
+                product(acc_b[:, :HALF], l_codes, l_scales, wa_codes[:, HALF:], wa_scales[:, HALF:])
+                nc.scalar.activation(y_win[0][:, :HALF], acc_a[:, :HALF], ACT.Copy, scale=gt_abs[:, 0:1])
+                nc.vector.tensor_scalar(y_win[0][:, HALF:W], acc_b[:, :HALF], gt_abs[:, 0:1], None, ALU.mult)
+            else:
+                acc = ps.tile([P, W], F32, name="acc_y%d" % t, tag="bank%d" % t)
+                product(acc[:], l_codes, l_scales, wa_codes[:], wa_scales[:])
+                nc.scalar.activation(y_win[t][:, :W], acc[:], ACT.Copy, scale=gt_abs[:, t : t + 1])
+            nc.scalar.copy(y_bf[:, t, :], y_win[t][:, :W])
+
+        w1_bf = sb.tile([P, PACK, W], BF16, name="w1_bf", align_bytes=64)
+        for j in range(PACK):
+            nc.scalar.activation(
+                w1_bf[:, j, :].rearrange("p (t b e) -> p b t e", t=PACK, e=8),
+                w1_raw[:, j, :].rearrange("p (b t e) -> p b t e", t=PACK, e=8),
+                ACT.Copy, scale=gt_sign[:, j : j + 1],
+            )
+        w1_grouped = sb.tile([P, W, PACK], BF16, name="w1_grouped", tag="hold_w1", align_bytes=64)
+        interleave(nc.scalar.copy, w1_grouped[:], w1_bf[:])
+        w1_codes = sb.tile([P, W], U32, name="w1_codes", align_bytes=64)
+        w1_scales = sb.tile([P, W], U8, name="w1_scales", align_bytes=64)
+
+        z_rows = sb.tile([P, PACK, W], BF16, name="z_rows", align_bytes=64)
+        z_codes = sb.tile([P, W], U32, name="z_codes", align_bytes=64)
+        z_scales = sb.tile([P, W], U8, name="z_scales", align_bytes=64)
+        steps = [(t, 0, W) for t in range(3)] + [(3, c0, c1) for c0, c1 in Z_CHUNKS]
+        at_n2, larger, z_grouped = {}, {}, {}
+
+        def piece(name, i, tag=None):
+            t, c0, c1 = steps[i]
+            name = "%s%d" % (name, i)
+            return sb.tile([P, c1 - c0], BF16, name=name, tag=tag or name, align_bytes=64)
+
+        def take_min(i):
+            t, c0, c1 = steps[i]
+            nc.vector.tensor_tensor(z_rows[:, t, c0:c1], larger[i][:], at_n2[i][:], ALU.min)
+
+        def group_z(k, engine_copy, tag):
+            c0, c1 = Z_CHUNKS[k]
+            z_grouped[k] = sb.tile([P, c1 - c0, PACK], BF16, name="z_grouped%d" % k, tag=tag, align_bytes=64)
+            interleave(engine_copy, z_grouped[k][:], z_rows[:, :, c0:c1])
+
+        def quantize_z(k):
+            c0, c1 = Z_CHUNKS[k]
+            quantize(z_codes[:, c0:c1], z_scales[:, c0:c1], z_grouped[k][:])
+
+        for i, (t, c0, c1) in enumerate(steps):
+            if i == 4:
+                quantize(w1_codes[:], w1_scales[:], w1_grouped[:])
+            at_n1 = piece("at_n1", i, "hold_w1" if i == 4 else None)
+            nc.vector.tensor_copy(at_n1[:], y_win[t][:].indirect(entries(n1_t, c0, c1)))
+            if i > 0:
+                take_min(i - 1)
+            if i == 4:
+                group_z(0, nc.scalar.copy, "hold_z0")
+            if i == 5:
+                group_z(1, nc.scalar.copy, "hold_z1")
+            at_n2[i] = piece("at_n2", i)
+            nc.vector.tensor_copy(at_n2[i][:], y_win[t][:].indirect(entries(n2_t, c0, c1)))
+            if i == 5:
+                quantize_z(0)
+            larger[i] = piece("larger", i, "hold_z0" if i == 5 else None)
+            nc.vector.tensor_tensor(larger[i][:], at_n1[:], y_bf[:, t, c0:c1], ALU.max)
+        take_min(5)
+        quantize_z(1)
+        group_z(2, nc.vector.tensor_copy, "hold_z1")
+
+        h_win = [sb.tile([P, W], F32, name="h_win%d" % t) for t in range(PACK)]
+        h0_copy = sb.tile([P, W], F32, name="h0_copy")
+        l_codes, l_scales = w1_codes[:, :P], w1_scales[:, :P]
+        acc_ab = ps.tile([P, W], F32, name="acc_ab", tag="bank0")
+        for k in range(2):
+            c0, c1 = Z_CHUNKS[k]
+            product(acc_ab[:, c0:c1], l_codes, l_scales, z_codes[:, c0:c1], z_scales[:, c0:c1])
+        c0, c1 = Z_CHUNKS[2]
+        nc.scalar.copy(h_win[0][:, :c0], acc_ab[:, :c0])
+        nc.scalar.copy(h0_copy[:, :HALF], acc_ab[:, :HALF])
+        quantize_z(2)
+        acc_c = ps.tile([P, W], F32, name="acc_c", tag="bank4")
+        product(acc_c[:, : c1 - c0], l_codes, l_scales, z_codes[:, c0:c1], z_scales[:, c0:c1])
+        nc.scalar.copy(h_win[0][:, c0:], acc_c[:, : c1 - c0])
+        acc_h = [None]
+        for t in range(1, PACK):
+            acc = ps.tile([P, W], F32, name="acc_h%d" % t, tag="bank%d" % t)
+            product(acc[:], w1_codes[:, t * P : (t + 1) * P], w1_scales[:, t * P : (t + 1) * P], z_codes[:], z_scales[:])
+            acc_h.append(acc)
+
+        out_rows = out.rearrange("(b t e) n -> t b e n", t=PACK, e=8)
+        gate = sb.tile([P, PACK, W], F32, name="gate")
+        term_a = sb.tile([P, PACK, W], F32, name="term_a")
+        term_b = sb.tile([P, PACK, W], F32, name="term_b")
+        result = sb.tile([P, PACK, W], F32, name="result")
+        halves = ((0, HALF), (HALF, W))
+
+        def sigmoid_at_n3(t, c0, c1):
+            nc.scalar.activation(gate[:, t, c0:c1], h_win[t][:].indirect(entries(n3_t, c0, c1)), ACT.Sigmoid)
+
+        def store(t, c0, c1):
+            nc.sync.dma_start(out_rows[t][:, :, c0:c1], result[:, t, c0:c1])
+
+        sigmoid_at_n3(0, 0, HALF)
+        nc.scalar.copy(h0_copy[:, HALF:], h_win[0][:, HALF:])
+        sigmoid_at_n3(0, HALF, W)
+        for c0, c1 in halves:
+            nc.vector.tensor_tensor(
+                term_a[:, 0, c0:c1], h_win[0][:].indirect(entries(n4_t, c0, c1)), h0_copy[:, c0:c1], ALU.subtract
+            )
+        for c0, c1 in halves:
+            nc.vector.tensor_tensor(term_b[:, 0, c0:c1], term_a[:, 0, c0:c1], gate[:, 0, c0:c1], ALU.mult)
+        for c0, c1 in halves:
+            nc.vector.tensor_tensor(result[:, 0, c0:c1], term_b[:, 0, c0:c1], h_win[0][:, c0:c1], ALU.add)
+        store(0, 0, W)
+
+        def finish(t, c0, c1):
+            nc.vector.tensor_tensor(result[:, t, c0:c1], term_a[:, t, c0:c1], term_b[:, t, c0:c1], ALU.subtract)
+            store(t, c0, c1)
+
+        pieces = [(t, c0, c1) for t in range(1, PACK) for c0, c1 in halves]
+        for i, (t, c0, c1) in enumerate(pieces):
+            if c0 == 0:
+                nc.scalar.copy(h_win[t][:], acc_h[t][:])
+            sigmoid_at_n3(t, c0, c1)
+            nc.vector.scalar_tensor_tensor(
+                term_b[:, t, c0:c1], gate[:, t, c0:c1], 1.0, h_win[t][:, c0:c1], ALU.subtract, ALU.mult
+            )
+            nc.vector.tensor_tensor(
+                term_a[:, t, c0:c1], h_win[t][:].indirect(entries(n4_t, c0, c1)), gate[:, t, c0:c1], ALU.mult
+            )
+            if i > 0:
+                finish(*pieces[i - 1])
+        finish(*pieces[-1])

@@ -57,25 +57,25 @@ def tile_picked_tokminmxtrack_none_p_kernel(tc, x_words, x_scales, wa, gt, w1, o
         warm = sb.tile([P, 8], F32, name="warm")
         nc.gpsimd.memset(warm[:], 0.0)
         nc.scalar.activation(warm[:, 4:8], warm[:, 0:4], ACT.Sigmoid)
-        y_win = [sb.tile([P, 2 * W if t < 3 else W], F32, name="y_win%d" % t) for t in range(PACK)]
-        for t in range(3):
+        y_win = [sb.tile([P, 2 * W if t < 2 else W], F32, name="y_win%d" % t) for t in range(PACK)]
+        for t in range(2):
             nc.vector.memset(y_win[t][:, W:], 0.0)
 
         offs_t = load_list(offs, "offs_t")
         gt_t = sb.tile([P, PACK], F32, name="gt_t")
-        nc.sync.dma_start(gt_t[:], gt.rearrange("(p t) o -> p (t o)", t=PACK))
+        nc.scalar.dma_start(gt_t[:], gt.rearrange("(p t) o -> p (t o)", t=PACK))
         for q in range(4):
             nc.scalar.dma_start(
                 x_bytes[32 * q : 32 * q + 4, :].bitcast(I32), x_scales[0, 4 * q : 4 * q + 4, :].bitcast(I32)
             )
+        x_codes = sb.tile([P, T], U32, name="x_codes", align_bytes=64)
+        nc.sync.dma_start(x_codes[:].bitcast(I32), x_words[0].rearrange("p n t -> p (n t)").bitcast(I32))
         wa_rows = wa.rearrange("(p j) n -> p j n", j=PACK)
         wa_raw = []
         for u in range(2):
             raw = sb.tile([P, PACK, HALF], F32, name="wa_raw%d" % u)
             nc.sync.dma_start(raw[:], wa_rows[:, :, u * HALF : (u + 1) * HALF])
             wa_raw.append(raw)
-        x_codes = sb.tile([P, T], U32, name="x_codes", align_bytes=64)
-        nc.sync.dma_start(x_codes[:].bitcast(I32), x_words[0].rearrange("p n t -> p (n t)").bitcast(I32))
         n1_t = load_list(n1, "n1_t")
         n2_t = load_list(n2, "n2_t")
         w1_raw = sb.tile([P, PACK, W], F32, name="w1_raw")
@@ -97,151 +97,182 @@ def tile_picked_tokminmxtrack_none_p_kernel(tc, x_words, x_scales, wa, gt, w1, o
             tok_scales[:].rearrange("p (t m) -> p t m", t=PACK), picked_bytes[:].rearrange("p (m t) -> p t m", t=PACK)
         )
 
-        wa_codes = sb.tile([P, W], U32, name="wa_codes", align_bytes=64)
-        wa_scales = sb.tile([P, W], U8, name="wa_scales", align_bytes=64)
-        for u in range(2):
-            grouped = sb.tile([P, HALF, PACK], BF16, name="wa_grouped%d" % u, align_bytes=64)
-            interleave(nc.scalar.copy, grouped[:], wa_raw[u][:])
-            quantize(wa_codes[:, u * HALF : (u + 1) * HALF], wa_scales[:, u * HALF : (u + 1) * HALF], grouped[:])
-
         tok_codes = sb.tile([P, W], U32, name="tok_codes", align_bytes=64)
         nc.vector.tensor_copy(tok_codes[:].rearrange("p (t m) -> p m t", t=PACK), x_codes[:].indirect(offs_t[:]))
 
-        y_bf = sb.tile([P, PACK, W], BF16, name="y_bf", align_bytes=64)
+        wa_codes = sb.tile([P, W], U32, name="wa_codes", align_bytes=64)
+        wa_scales = sb.tile([P, W], U8, name="wa_scales", align_bytes=64)
+        wa_grouped = []
+        for k, (c0, c1) in enumerate(Z_CHUNKS):
+            grouped = sb.tile([P, c1 - c0, PACK], BF16, name="wa_grouped%d" % k, align_bytes=64)
+            engine_copy = nc.vector.tensor_copy if k == 1 else nc.scalar.copy
+            interleave(engine_copy, grouped[:], wa_raw[c0 // HALF][:, :, c0 % HALF : c0 % HALF + c1 - c0])
+            wa_grouped.append(grouped)
+            if k == 0:
+                quantize(wa_codes[:, c0:c1], wa_scales[:, c0:c1], grouped[:])
+        for k in (1, 2):
+            c0, c1 = Z_CHUNKS[k]
+            quantize(wa_codes[:, c0:c1], wa_scales[:, c0:c1], wa_grouped[k][:])
+
+        lanes = sb.tile([P, 3, PACK, W], BF16, name="lanes", align_bytes=64)
+        fetched = lanes[:, 0:2, :, :].rearrange("p u (v n) c -> p (u v) n c", n=2)
+        at_n1 = fetched[:, :, 0, :]
+        at_n2 = fetched[:, :, 1, :]
+        y_bf = lanes[:, 1:3, :, HALF:]
         for t in range(PACK):
             l_codes = tok_codes[:, t * P : (t + 1) * P]
             l_scales = tok_scales[:, t * P : (t + 1) * P]
             if t == 0:
-                acc_a = ps.tile([P, W], F32, name="acc_a", tag="bank0")
-                acc_b = ps.tile([P, W], F32, name="acc_b", tag="bank4")
-                product(acc_a[:, :HALF], l_codes, l_scales, wa_codes[:, :HALF], wa_scales[:, :HALF])
-                product(acc_b[:, :HALF], l_codes, l_scales, wa_codes[:, HALF:], wa_scales[:, HALF:])
-                nc.scalar.activation(y_win[0][:, :HALF], acc_a[:, :HALF], ACT.Copy, scale=gt_abs[:, 0:1])
-                nc.vector.tensor_scalar(y_win[0][:, HALF:W], acc_b[:, :HALF], gt_abs[:, 0:1], None, ALU.mult)
+                for k, (c0, c1) in enumerate(Z_CHUNKS):
+                    acc = ps.tile([P, W], F32, name="acc_y0%d" % k, tag=("bank0", "bank4", "bank5")[k])
+                    product(acc[:, : c1 - c0], l_codes, l_scales, wa_codes[:, c0:c1], wa_scales[:, c0:c1])
+                    if k == 1:
+                        nc.vector.tensor_scalar(y_win[0][:, c0:c1], acc[:, : c1 - c0], gt_abs[:, 0:1], None, ALU.mult)
+                    else:
+                        nc.scalar.activation(y_win[0][:, c0:c1], acc[:, : c1 - c0], ACT.Copy, scale=gt_abs[:, 0:1])
             else:
                 acc = ps.tile([P, W], F32, name="acc_y%d" % t, tag="bank%d" % t)
                 product(acc[:], l_codes, l_scales, wa_codes[:], wa_scales[:])
-                nc.scalar.activation(y_win[t][:, :W], acc[:], ACT.Copy, scale=gt_abs[:, t : t + 1])
-            nc.scalar.copy(y_bf[:, t, :], y_win[t][:, :W])
+                if t < 3:
+                    nc.scalar.activation(y_win[t][:, :W], acc[:], ACT.Copy, scale=gt_abs[:, t : t + 1])
+                if t == 1:
+                    nc.scalar.copy(y_bf[:, :, 0, :], y_win[0][:, :W].rearrange("p (u c) -> p u c", u=2))
+                nc.scalar.activation(
+                    y_bf[:, :, t, :], acc[:].rearrange("p (u c) -> p u c", u=2), ACT.Copy, scale=gt_abs[:, t : t + 1]
+                )
+                if t == 3:
+                    nc.scalar.activation(y_win[t][:, :W], acc[:], ACT.Copy, scale=gt_abs[:, t : t + 1])
 
-        w1_bf = sb.tile([P, PACK, W], BF16, name="w1_bf", align_bytes=64)
+        w1_bf = sb.tile([P, PACK, W], BF16, name="w1_bf", tag="hold_z0", align_bytes=64)
         for j in range(PACK):
             nc.scalar.activation(
                 w1_bf[:, j, :].rearrange("p (t b e) -> p b t e", t=PACK, e=8),
                 w1_raw[:, j, :].rearrange("p (b t e) -> p b t e", t=PACK, e=8),
                 ACT.Copy, scale=gt_sign[:, j : j + 1],
             )
-        w1_grouped = sb.tile([P, W, PACK], BF16, name="w1_grouped", tag="hold_w1", align_bytes=64)
-        interleave(nc.scalar.copy, w1_grouped[:], w1_bf[:])
-        w1_codes = sb.tile([P, W], U32, name="w1_codes", align_bytes=64)
+        w1_grouped = []
+        for u in range(2):
+            grouped = sb.tile([P, HALF, PACK], BF16, name="w1_grouped%d" % u, align_bytes=64)
+            interleave(nc.scalar.copy, grouped[:], w1_bf[:, :, u * HALF : (u + 1) * HALF])
+            w1_grouped.append(grouped)
+        w1_codes_lo = sb.tile([P, HALF], U32, name="w1_codes_lo", align_bytes=64)
         w1_scales = sb.tile([P, W], U8, name="w1_scales", align_bytes=64)
 
-        z_rows = sb.tile([P, PACK, W], BF16, name="z_rows", align_bytes=64)
+        halves = ((0, HALF), (HALF, W))
+        larger = [sb.tile([P, PACK, c1 - c0], BF16, name="larger%d" % c0, align_bytes=64) for c0, c1 in Z_CHUNKS]
+        z_rows = [sb.tile([P, PACK, c1 - c0], BF16, name="z_rows%d" % c0, align_bytes=64) for c0, c1 in Z_CHUNKS]
         z_codes = sb.tile([P, W], U32, name="z_codes", align_bytes=64)
         z_scales = sb.tile([P, W], U8, name="z_scales", align_bytes=64)
-        steps = [(t, 0, W) for t in range(3)] + [(3, c0, c1) for c0, c1 in Z_CHUNKS]
-        at_n2, larger, z_grouped = {}, {}, {}
+        z_grouped = sb.tile([P, W, PACK], BF16, name="z_grouped", tag="hold_z0", align_bytes=64)
 
-        def piece(name, i, tag=None):
-            t, c0, c1 = steps[i]
-            name = "%s%d" % (name, i)
-            return sb.tile([P, c1 - c0], BF16, name=name, tag=tag or name, align_bytes=64)
+        def fetch(dst, lst, t, c0, c1):
+            nc.vector.tensor_copy(dst[:, t, c0:c1], y_win[t][:].indirect(entries(lst, c0, c1)))
 
-        def take_min(i):
-            t, c0, c1 = steps[i]
-            nc.vector.tensor_tensor(z_rows[:, t, c0:c1], larger[i][:], at_n2[i][:], ALU.min)
-
-        def group_z(k, engine_copy, tag):
+        def take_min(k):
             c0, c1 = Z_CHUNKS[k]
-            z_grouped[k] = sb.tile([P, c1 - c0, PACK], BF16, name="z_grouped%d" % k, tag=tag, align_bytes=64)
-            interleave(engine_copy, z_grouped[k][:], z_rows[:, :, c0:c1])
+            nc.vector.tensor_tensor(z_rows[k][:], larger[k][:], at_n2[:, :, c0:c1], ALU.min)
+            interleave(nc.scalar.copy, z_grouped[:, c0:c1, :], z_rows[k][:])
 
-        def quantize_z(k):
-            c0, c1 = Z_CHUNKS[k]
-            quantize(z_codes[:, c0:c1], z_scales[:, c0:c1], z_grouped[k][:])
-
-        for i, (t, c0, c1) in enumerate(steps):
-            if i == 4:
-                quantize(w1_codes[:], w1_scales[:], w1_grouped[:])
-            at_n1 = piece("at_n1", i, "hold_w1" if i == 4 else None)
-            nc.vector.tensor_copy(at_n1[:], y_win[t][:].indirect(entries(n1_t, c0, c1)))
-            if i > 0:
-                take_min(i - 1)
-            if i == 4:
-                group_z(0, nc.scalar.copy, "hold_z0")
-            if i == 5:
-                group_z(1, nc.scalar.copy, "hold_z1")
-            at_n2[i] = piece("at_n2", i)
-            nc.vector.tensor_copy(at_n2[i][:], y_win[t][:].indirect(entries(n2_t, c0, c1)))
-            if i == 5:
-                quantize_z(0)
-            larger[i] = piece("larger", i, "hold_z0" if i == 5 else None)
-            nc.vector.tensor_tensor(larger[i][:], at_n1[:], y_bf[:, t, c0:c1], ALU.max)
-        take_min(5)
-        quantize_z(1)
-        group_z(2, nc.vector.tensor_copy, "hold_z1")
+        for t in range(2):
+            fetch(at_n1, n1_t, t, 0, W)
+            fetch(at_n2, n2_t, t, 0, W)
+        for k, (c0, c1) in enumerate(Z_CHUNKS):
+            if k < 2:
+                fetch(at_n1, n1_t, 2, *halves[k])
+            if k == 1:
+                take_min(0)
+            if k < 2:
+                fetch(at_n2, n2_t, 2, *halves[k])
+            fetch(at_n1, n1_t, 3, c0, c1)
+            if k == 2:
+                take_min(1)
+            fetch(at_n2, n2_t, 3, c0, c1)
+            nc.vector.tensor_tensor(
+                larger[k][:], at_n1[:, :, c0:c1], y_bf[:, c0 // HALF, :, c0 % HALF : c0 % HALF + c1 - c0], ALU.max
+            )
+        take_min(2)
+        quantize(w1_codes_lo[:], w1_scales[:, :HALF], w1_grouped[0][:])
+        for k, (c0, c1) in enumerate(Z_CHUNKS):
+            quantize(z_codes[:, c0:c1], z_scales[:, c0:c1], z_grouped[:, c0:c1, :])
 
         h_win = [sb.tile([P, W], F32, name="h_win%d" % t) for t in range(PACK)]
-        h0_copy = sb.tile([P, W], F32, name="h0_copy")
-        l_codes, l_scales = w1_codes[:, :P], w1_scales[:, :P]
-        acc_ab = ps.tile([P, W], F32, name="acc_ab", tag="bank0")
-        for k in range(2):
-            c0, c1 = Z_CHUNKS[k]
-            product(acc_ab[:, c0:c1], l_codes, l_scales, z_codes[:, c0:c1], z_scales[:, c0:c1])
-        c0, c1 = Z_CHUNKS[2]
-        nc.scalar.copy(h_win[0][:, :c0], acc_ab[:, :c0])
-        nc.scalar.copy(h0_copy[:, :HALF], acc_ab[:, :HALF])
-        quantize_z(2)
-        acc_c = ps.tile([P, W], F32, name="acc_c", tag="bank4")
-        product(acc_c[:, : c1 - c0], l_codes, l_scales, z_codes[:, c0:c1], z_scales[:, c0:c1])
-        nc.scalar.copy(h_win[0][:, c0:], acc_c[:, : c1 - c0])
-        acc_h = [None]
-        for t in range(1, PACK):
-            acc = ps.tile([P, W], F32, name="acc_h%d" % t, tag="bank%d" % t)
-            product(acc[:], w1_codes[:, t * P : (t + 1) * P], w1_scales[:, t * P : (t + 1) * P], z_codes[:], z_scales[:])
-            acc_h.append(acc)
+        h0_copy = sb.tile([P, HALF], F32, name="h0_copy")
+        l_codes, l_scales = w1_codes_lo[:, :P], w1_scales[:, :P]
+        acc_lo = ps.tile([P, W], F32, name="acc_lo", tag="bank0")
+        product(acc_lo[:, :HALF], l_codes, l_scales, z_codes[:, :HALF], z_scales[:, :HALF])
+        acc_hi = []
+        for c0, c1 in Z_CHUNKS[1:]:
+            acc = ps.tile([P, W], F32, name="acc_hi%d" % c0, tag="bank%d" % (4 if c0 == HALF else 6))
+            product(acc[:, :P], l_codes, l_scales, z_codes[:, c0:c1], z_scales[:, c0:c1])
+            acc_hi.append(acc)
+        nc.scalar.copy(h_win[0][:, :HALF], acc_lo[:, :HALF])
+        nc.scalar.copy(h0_copy[:], acc_lo[:, :HALF])
+        for u, (c0, c1) in enumerate(halves):
+            acc = ps.tile([P, W], F32, name="acc_h1%d" % u, tag=("bank1", "bank5")[u])
+            product(acc[:, :HALF], w1_codes_lo[:, P:], w1_scales[:, P:HALF], z_codes[:, c0:c1], z_scales[:, c0:c1])
+            nc.scalar.copy(h_win[1][:, c0:c1], acc[:, :HALF])
+        w1_codes_hi = sb.tile([P, HALF], U32, name="w1_codes_hi", tag="hold_z0", align_bytes=64)
+        quantize(w1_codes_hi[:], w1_scales[:, HALF:], w1_grouped[1][:])
+        for acc, (c0, c1) in zip(acc_hi, Z_CHUNKS[1:]):
+            nc.vector.tensor_copy(h_win[0][:, c0:c1], acc[:, :P])
 
         out_rows = out.rearrange("(b t e) n -> t b e n", t=PACK, e=8)
         gate = sb.tile([P, PACK, W], F32, name="gate")
         term_a = sb.tile([P, PACK, W], F32, name="term_a")
         term_b = sb.tile([P, PACK, W], F32, name="term_b")
         result = sb.tile([P, PACK, W], F32, name="result")
-        halves = ((0, HALF), (HALF, W))
+
+        def h_rows(t):
+            acc = ps.tile([P, W], F32, name="acc_h%d" % t, tag="bank%d" % t)
+            product(acc[:], w1_codes_hi[:, t % 2 * P : (t % 2 + 1) * P], w1_scales[:, t * P : (t + 1) * P], z_codes[:], z_scales[:])
+            nc.scalar.copy(h_win[t][:], acc[:])
 
         def sigmoid_at_n3(t, c0, c1):
             nc.scalar.activation(gate[:, t, c0:c1], h_win[t][:].indirect(entries(n3_t, c0, c1)), ACT.Sigmoid)
 
-        def store(t, c0, c1):
-            nc.sync.dma_start(out_rows[t][:, :, c0:c1], result[:, t, c0:c1])
-
-        sigmoid_at_n3(0, 0, HALF)
-        nc.scalar.copy(h0_copy[:, HALF:], h_win[0][:, HALF:])
-        sigmoid_at_n3(0, HALF, W)
-        for c0, c1 in halves:
+        def gated_at_n4(t, c0, c1):
             nc.vector.tensor_tensor(
-                term_a[:, 0, c0:c1], h_win[0][:].indirect(entries(n4_t, c0, c1)), h0_copy[:, c0:c1], ALU.subtract
+                term_a[:, t, c0:c1], h_win[t][:].indirect(entries(n4_t, c0, c1)), gate[:, t, c0:c1], ALU.mult
             )
-        for c0, c1 in halves:
-            nc.vector.tensor_tensor(term_b[:, 0, c0:c1], term_a[:, 0, c0:c1], gate[:, 0, c0:c1], ALU.mult)
-        for c0, c1 in halves:
-            nc.vector.tensor_tensor(result[:, 0, c0:c1], term_b[:, 0, c0:c1], h_win[0][:, c0:c1], ALU.add)
-        store(0, 0, W)
+
+        def gated_in_place(t, c0, c1):
+            nc.vector.scalar_tensor_tensor(
+                term_b[:, t, c0:c1], gate[:, t, c0:c1], 1.0, h_win[t][:, c0:c1], ALU.subtract, ALU.mult
+            )
+
+        def store(t, c0, c1):
+            queue = nc.scalar if (t, c1) == (PACK - 1, W) else nc.sync
+            queue.dma_start(out_rows[t][:, :, c0:c1], result[:, t, c0:c1])
 
         def finish(t, c0, c1):
             nc.vector.tensor_tensor(result[:, t, c0:c1], term_a[:, t, c0:c1], term_b[:, t, c0:c1], ALU.subtract)
             store(t, c0, c1)
 
-        pieces = [(t, c0, c1) for t in range(1, PACK) for c0, c1 in halves]
-        for i, (t, c0, c1) in enumerate(pieces):
-            if c0 == 0:
-                nc.scalar.copy(h_win[t][:], acc_h[t][:])
-            sigmoid_at_n3(t, c0, c1)
-            nc.vector.scalar_tensor_tensor(
-                term_b[:, t, c0:c1], gate[:, t, c0:c1], 1.0, h_win[t][:, c0:c1], ALU.subtract, ALU.mult
-            )
-            nc.vector.tensor_tensor(
-                term_a[:, t, c0:c1], h_win[t][:].indirect(entries(n4_t, c0, c1)), gate[:, t, c0:c1], ALU.mult
-            )
-            if i > 0:
-                finish(*pieces[i - 1])
-        finish(*pieces[-1])
+        lo, hi = halves
+        sigmoid_at_n3(0, *hi)
+        sigmoid_at_n3(0, *lo)
+        nc.vector.tensor_tensor(term_a[:, 0, :HALF], h_win[0][:].indirect(entries(n4_t, *lo)), h0_copy[:], ALU.subtract)
+        gated_at_n4(0, *hi)
+        nc.vector.tensor_tensor(term_b[:, 0, :HALF], term_a[:, 0, :HALF], gate[:, 0, :HALF], ALU.mult)
+        gated_in_place(0, *hi)
+        nc.vector.tensor_tensor(result[:, 0, :HALF], term_b[:, 0, :HALF], h0_copy[:], ALU.add)
+        store(0, *lo)
+        finish(0, *hi)
+
+        for t in range(1, PACK):
+            sigmoid_at_n3(t, *lo)
+            if t < 3:
+                h_rows(t + 1)
+            sigmoid_at_n3(t, *hi)
+            gated_at_n4(t, *lo)
+            if t == 3:
+                gated_in_place(3, 0, W)
+            if t > 1:
+                finish(t - 1, 0, W)
+            if t < 3:
+                gated_at_n4(t, *hi)
+                gated_in_place(t, 0, W)
+        for k in (1, 2):
+            gated_at_n4(3, *Z_CHUNKS[k])
+            finish(3, *Z_CHUNKS[k - 1])
+        finish(3, *Z_CHUNKS[2])

@@ -55,21 +55,21 @@ def tile_picked_tokminmxtrack_none_p_kernel(tc, x_words, x_scales, wa, gt, w1, o
         x_bytes = sb.tile([P, T], U8, name="x_bytes", align_bytes=64)
         nc.vector.memset(x_bytes[:].bitcast(I32), 0)
         warm = sb.tile([P, 8], F32, name="warm")
-        nc.gpsimd.memset(warm[:], 0.0)
-        nc.scalar.activation(warm[:, 4:8], warm[:, 0:4], ACT.Sigmoid)
+        nc.vector.memset(warm[:, 0:4], 0.0)
         y_win = [sb.tile([P, 2 * W if t < 2 else W], F32, name="y_win%d" % t) for t in range(PACK)]
         for t in range(2):
             nc.vector.memset(y_win[t][:, W:], 0.0)
 
         offs_t = load_list(offs, "offs_t")
-        gt_t = sb.tile([P, PACK], F32, name="gt_t")
-        nc.scalar.dma_start(gt_t[:], gt.rearrange("(p t) o -> p (t o)", t=PACK))
         for q in range(4):
             nc.scalar.dma_start(
                 x_bytes[32 * q : 32 * q + 4, :].bitcast(I32), x_scales[0, 4 * q : 4 * q + 4, :].bitcast(I32)
             )
         x_codes = sb.tile([P, T], U32, name="x_codes", align_bytes=64)
         nc.sync.dma_start(x_codes[:].bitcast(I32), x_words[0].rearrange("p n t -> p (n t)").bitcast(I32))
+        gt_t = sb.tile([P, PACK], F32, name="gt_t")
+        nc.scalar.dma_start(gt_t[:], gt.rearrange("(p t) o -> p (t o)", t=PACK))
+        nc.scalar.activation(warm[:, 4:8], warm[:, 0:4], ACT.Sigmoid)
         wa_rows = wa.rearrange("(p j) n -> p j n", j=PACK)
         wa_raw = []
         for u in range(2):
@@ -199,12 +199,10 @@ def tile_picked_tokminmxtrack_none_p_kernel(tc, x_words, x_scales, wa, gt, w1, o
         h0_copy = sb.tile([P, HALF], F32, name="h0_copy")
         l_codes, l_scales = w1_codes_lo[:, :P], w1_scales[:, :P]
         acc_lo = ps.tile([P, W], F32, name="acc_lo", tag="bank0")
+        acc_hi = ps.tile([P, W], F32, name="acc_hi", tag="bank4")
         product(acc_lo[:, :HALF], l_codes, l_scales, z_codes[:, :HALF], z_scales[:, :HALF])
-        acc_hi = []
         for c0, c1 in Z_CHUNKS[1:]:
-            acc = ps.tile([P, W], F32, name="acc_hi%d" % c0, tag="bank%d" % (4 if c0 == HALF else 6))
-            product(acc[:, :P], l_codes, l_scales, z_codes[:, c0:c1], z_scales[:, c0:c1])
-            acc_hi.append(acc)
+            product(acc_hi[:, c0 - HALF : c1 - HALF], l_codes, l_scales, z_codes[:, c0:c1], z_scales[:, c0:c1])
         nc.scalar.copy(h_win[0][:, :HALF], acc_lo[:, :HALF])
         nc.scalar.copy(h0_copy[:], acc_lo[:, :HALF])
         for u, (c0, c1) in enumerate(halves):
@@ -213,8 +211,7 @@ def tile_picked_tokminmxtrack_none_p_kernel(tc, x_words, x_scales, wa, gt, w1, o
             nc.scalar.copy(h_win[1][:, c0:c1], acc[:, :HALF])
         w1_codes_hi = sb.tile([P, HALF], U32, name="w1_codes_hi", tag="hold_z0", align_bytes=64)
         quantize(w1_codes_hi[:], w1_scales[:, HALF:], w1_grouped[1][:])
-        for acc, (c0, c1) in zip(acc_hi, Z_CHUNKS[1:]):
-            nc.vector.tensor_copy(h_win[0][:, c0:c1], acc[:, :P])
+        nc.vector.tensor_copy(h_win[0][:, HALF:], acc_hi[:, :HALF])
 
         out_rows = out.rearrange("(b t e) n -> t b e n", t=PACK, e=8)
         gate = sb.tile([P, PACK, W], F32, name="gate")

@@ -53,7 +53,7 @@ def tile_picked_tokminmxtrack_none_p_kernel(tc, x_words, x_scales, wa, gt, w1, o
             )
 
         x_bytes = sb.tile([P, T], U8, name="x_bytes", align_bytes=64)
-        nc.vector.memset(x_bytes[:].bitcast(I32), 0)
+        nc.gpsimd.memset(x_bytes[:].bitcast(I32), 0)
         warm = sb.tile([P, 8], F32, name="warm")
         nc.vector.memset(warm[:, 0:4], 0.0)
         y_win = [sb.tile([P, 2 * W if t < 2 else W], F32, name="y_win%d" % t) for t in range(PACK)]
@@ -61,12 +61,12 @@ def tile_picked_tokminmxtrack_none_p_kernel(tc, x_words, x_scales, wa, gt, w1, o
             nc.vector.memset(y_win[t][:, W:], 0.0)
 
         offs_t = load_list(offs, "offs_t")
-        for q in range(4):
-            nc.scalar.dma_start(
-                x_bytes[32 * q : 32 * q + 4, :].bitcast(I32), x_scales[0, 4 * q : 4 * q + 4, :].bitcast(I32)
-            )
         x_codes = sb.tile([P, T], U32, name="x_codes", align_bytes=64)
         nc.sync.dma_start(x_codes[:].bitcast(I32), x_words[0].rearrange("p n t -> p (n t)").bitcast(I32))
+        for q in range(4):
+            nc.sync.dma_start(
+                x_bytes[32 * q : 32 * q + 4, :].bitcast(I32), x_scales[0, 4 * q : 4 * q + 4, :].bitcast(I32)
+            )
         gt_t = sb.tile([P, PACK], F32, name="gt_t")
         nc.scalar.dma_start(gt_t[:], gt.rearrange("(p t) o -> p (t o)", t=PACK))
         nc.scalar.activation(warm[:, 4:8], warm[:, 0:4], ACT.Sigmoid)
@@ -90,15 +90,15 @@ def tile_picked_tokminmxtrack_none_p_kernel(tc, x_words, x_scales, wa, gt, w1, o
         gt_abs = sb.tile([P, PACK], F32, name="gt_abs")
         nc.gpsimd.tensor_tensor(gt_abs[:], gt_t[:], gt_sign[:], ALU.mult)
 
+        tok_codes = sb.tile([P, W], U32, name="tok_codes", align_bytes=64)
+        nc.vector.tensor_copy(tok_codes[:].rearrange("p (t m) -> p m t", t=PACK), x_codes[:].indirect(offs_t[:]))
+
         picked_bytes = sb.tile([P, W], U8, name="picked_bytes", align_bytes=64)
         nc.vector.tensor_copy(picked_bytes[:], x_bytes[:].indirect(offs_t[:]))
         tok_scales = sb.tile([P, W], U8, name="tok_scales", align_bytes=64)
         nc.vector.tensor_copy(
             tok_scales[:].rearrange("p (t m) -> p t m", t=PACK), picked_bytes[:].rearrange("p (m t) -> p t m", t=PACK)
         )
-
-        tok_codes = sb.tile([P, W], U32, name="tok_codes", align_bytes=64)
-        nc.vector.tensor_copy(tok_codes[:].rearrange("p (t m) -> p m t", t=PACK), x_codes[:].indirect(offs_t[:]))
 
         wa_codes = sb.tile([P, W], U32, name="wa_codes", align_bytes=64)
         wa_scales = sb.tile([P, W], U8, name="wa_scales", align_bytes=64)

from contextlib import ExitStack

import concourse.mybir as mybir

FLOPS = 2 * 2 * 512 * 512 * 512

F32 = mybir.dt.float32
BF16 = mybir.dt.bfloat16
I32 = mybir.dt.int32
U32 = mybir.dt.uint32
U16 = mybir.dt.uint16
U8 = mybir.dt.uint8
FP8X4 = mybir.dt.float8_e4m3fn_x4
ALU = mybir.AluOpType
ACT = mybir.ActivationFunctionType

P = 128
PACK = 4
T = 2048
W = 512
HALF = 256
Z_CHUNKS = ((0, 256), (256, 384), (384, 512))


def tile_picked_tokminmxtrack_none_p_kernel(tc, x_words, x_scales, wa, gt, w1, offs, n1, n2, n3, n4, out):
    nc = tc.nc
    with ExitStack() as ctx:
        lists = ctx.enter_context(tc.tile_pool(name="lists", bufs=1))
        sb = ctx.enter_context(tc.tile_pool(name="sb", bufs=1))
        ps = ctx.enter_context(tc.psum_pool(name="ps", bufs=1))

        def load_list(src, name):
            tile = lists.tile([P, W // 16], U16, name=name)
            nc.sync.dma_start(tile[:], src)
            return tile

        def entries(tile, c0, c1):
            return tile[:, c0 // 16 : c1 // 16]

        def interleave(engine_copy, dst, src):
            engine_copy(
                dst.rearrange("p (c i) t -> p c t i", i=4),
                src.rearrange("p t (c i) -> p c t i", i=4),
            )

        def quantize(codes, scales, grouped):
            nc.vector.quantize_mx(out=codes.bitcast(FP8X4), scales=scales, in_=grouped.rearrange("p c t -> p (c t)"))

        def product(acc, l_codes, l_scales, r_codes, r_scales):
            nc.tensor.matmul_mx(
                out=acc, lhsT=l_codes.bitcast(FP8X4), lhsT_scale=l_scales,
                rhs=r_codes.bitcast(FP8X4), rhs_scale=r_scales, start=True, stop=True,
            )

        x_bytes = sb.tile([P, T], U8, name="x_bytes", align_bytes=64)
        nc.gpsimd.memset(x_bytes[:].bitcast(I32), 0)
        warm = sb.tile([P, 8], F32, name="warm")
        nc.vector.memset(warm[:, 0:4], 0.0)
        y_win = [sb.tile([P, 2 * W if t < 2 else W], F32, name="y_win%d" % t) for t in range(PACK)]
        for t in range(2):
            nc.vector.memset(y_win[t][:, W:], 0.0)

        offs_t = load_list(offs, "offs_t")
        x_codes = sb.tile([P, T], U32, name="x_codes", align_bytes=64)
        nc.sync.dma_start(x_codes[:].bitcast(I32), x_words[0].rearrange("p n t -> p (n t)").bitcast(I32))
        for q in range(4):
            nc.sync.dma_start(
                x_bytes[32 * q : 32 * q + 4, :].bitcast(I32), x_scales[0, 4 * q : 4 * q + 4, :].bitcast(I32)
            )
        gt_t = sb.tile([P, PACK], F32, name="gt_t")
        nc.scalar.dma_start(gt_t[:], gt.rearrange("(p t) o -> p (t o)", t=PACK))
        nc.scalar.activation(warm[:, 4:8], warm[:, 0:4], ACT.Sigmoid)
        wa_rows = wa.rearrange("(p j) n -> p j n", j=PACK)
        wa_raw = []
        for u in range(2):
            raw = sb.tile([P, PACK, HALF], F32, name="wa_raw%d" % u)
            nc.sync.dma_start(raw[:], wa_rows[:, :, u * HALF : (u + 1) * HALF])
            wa_raw.append(raw)
        n1_t = load_list(n1, "n1_t")
        n2_t = load_list(n2, "n2_t")
        w1_raw = sb.tile([P, PACK, W], F32, name="w1_raw")
        nc.sync.dma_start(w1_raw[:], w1.rearrange("(p j) n -> p j n", j=PACK))
        n3_t = load_list(n3, "n3_t")
        n4_t = load_list(n4, "n4_t")

        gt_pos = sb.tile([P, PACK], F32, name="gt_pos")
        nc.gpsimd.tensor_scalar(gt_pos[:], gt_t[:], 0.0, 2.0, ALU.is_ge, ALU.mult)
        gt_sign = sb.tile([P, PACK], F32, name="gt_sign")
        nc.gpsimd.tensor_scalar(gt_sign[:], gt_pos[:], 1.0, -1.0, ALU.mult, ALU.add)
        gt_abs = sb.tile([P, PACK], F32, name="gt_abs")
        nc.gpsimd.tensor_tensor(gt_abs[:], gt_t[:], gt_sign[:], ALU.mult)

        tok_codes = sb.tile([P, W], U32, name="tok_codes", align_bytes=64)
        nc.vector.tensor_copy(tok_codes[:].rearrange("p (t m) -> p m t", t=PACK), x_codes[:].indirect(offs_t[:]))

        picked_bytes = sb.tile([P, W], U8, name="picked_bytes", align_bytes=64)
        nc.vector.tensor_copy(picked_bytes[:], x_bytes[:].indirect(offs_t[:]))
        tok_scales = sb.tile([P, W], U8, name="tok_scales", align_bytes=64)
        nc.vector.tensor_copy(
            tok_scales[:].rearrange("p (t m) -> p t m", t=PACK), picked_bytes[:].rearrange("p (m t) -> p t m", t=PACK)
        )

        wa_codes = sb.tile([P, W], U32, name="wa_codes", align_bytes=64)
        wa_scales = sb.tile([P, W], U8, name="wa_scales", align_bytes=64)
        wa_grouped = []
        for k, (c0, c1) in enumerate(Z_CHUNKS):
            grouped = sb.tile([P, c1 - c0, PACK], BF16, name="wa_grouped%d" % k, align_bytes=64)
            engine_copy = nc.vector.tensor_copy if k == 1 else nc.scalar.copy
            interleave(engine_copy, grouped[:], wa_raw[c0 // HALF][:, :, c0 % HALF : c0 % HALF + c1 - c0])
            wa_grouped.append(grouped)
            if k == 0:
                quantize(wa_codes[:, c0:c1], wa_scales[:, c0:c1], grouped[:])
        for k in (1, 2):
            c0, c1 = Z_CHUNKS[k]
            quantize(wa_codes[:, c0:c1], wa_scales[:, c0:c1], wa_grouped[k][:])

        lanes = sb.tile([P, 3, PACK, W], BF16, name="lanes", align_bytes=64)
        fetched = lanes[:, 0:2, :, :].rearrange("p u (v n) c -> p (u v) n c", n=2)
        at_n1 = fetched[:, :, 0, :]
        at_n2 = fetched[:, :, 1, :]
        y_bf = lanes[:, 1:3, :, HALF:]
        for t in range(PACK):
            l_codes = tok_codes[:, t * P : (t + 1) * P]
            l_scales = tok_scales[:, t * P : (t + 1) * P]
            if t == 0:
                for k, (c0, c1) in enumerate(Z_CHUNKS):
                    acc = ps.tile([P, W], F32, name="acc_y0%d" % k, tag=("bank0", "bank4", "bank5")[k])
                    product(acc[:, : c1 - c0], l_codes, l_scales, wa_codes[:, c0:c1], wa_scales[:, c0:c1])
                    if k == 1:
                        nc.vector.tensor_scalar(y_win[0][:, c0:c1], acc[:, : c1 - c0], gt_abs[:, 0:1], None, ALU.mult)
                    else:
                        nc.scalar.activation(y_win[0][:, c0:c1], acc[:, : c1 - c0], ACT.Copy, scale=gt_abs[:, 0:1])
            else:
                acc = ps.tile([P, W], F32, name="acc_y%d" % t, tag="bank%d" % t)
                product(acc[:], l_codes, l_scales, wa_codes[:], wa_scales[:])
                if t < 3:
                    nc.scalar.activation(y_win[t][:, :W], acc[:], ACT.Copy, scale=gt_abs[:, t : t + 1])
                if t == 1:
                    nc.scalar.copy(y_bf[:, :, 0, :], y_win[0][:, :W].rearrange("p (u c) -> p u c", u=2))
                nc.scalar.activation(
                    y_bf[:, :, t, :], acc[:].rearrange("p (u c) -> p u c", u=2), ACT.Copy, scale=gt_abs[:, t : t + 1]
                )
                if t == 3:
                    nc.scalar.activation(y_win[t][:, :W], acc[:], ACT.Copy, scale=gt_abs[:, t : t + 1])

        w1_bf = sb.tile([P, PACK, W], BF16, name="w1_bf", tag="hold_z0", align_bytes=64)
        for j in range(PACK):
            nc.scalar.activation(
                w1_bf[:, j, :].rearrange("p (t b e) -> p b t e", t=PACK, e=8),
                w1_raw[:, j, :].rearrange("p (b t e) -> p b t e", t=PACK, e=8),
                ACT.Copy, scale=gt_sign[:, j : j + 1],
            )
        w1_grouped = []
        for u in range(2):
            grouped = sb.tile([P, HALF, PACK], BF16, name="w1_grouped%d" % u, align_bytes=64)
            interleave(nc.scalar.copy, grouped[:], w1_bf[:, :, u * HALF : (u + 1) * HALF])
            w1_grouped.append(grouped)
        w1_codes_lo = sb.tile([P, HALF], U32, name="w1_codes_lo", align_bytes=64)
        w1_scales = sb.tile([P, W], U8, name="w1_scales", align_bytes=64)

        halves = ((0, HALF), (HALF, W))
        larger = [sb.tile([P, PACK, c1 - c0], BF16, name="larger%d" % c0, align_bytes=64) for c0, c1 in Z_CHUNKS]
        z_rows = [sb.tile([P, PACK, c1 - c0], BF16, name="z_rows%d" % c0, align_bytes=64) for c0, c1 in Z_CHUNKS]
        z_codes = sb.tile([P, W], U32, name="z_codes", align_bytes=64)
        z_scales = sb.tile([P, W], U8, name="z_scales", align_bytes=64)
        z_grouped = sb.tile([P, W, PACK], BF16, name="z_grouped", tag="hold_z0", align_bytes=64)

        def fetch(dst, lst, t, c0, c1):
            nc.vector.tensor_copy(dst[:, t, c0:c1], y_win[t][:].indirect(entries(lst, c0, c1)))

        def take_min(k):
            c0, c1 = Z_CHUNKS[k]
            nc.vector.tensor_tensor(z_rows[k][:], larger[k][:], at_n2[:, :, c0:c1], ALU.min)
            interleave(nc.scalar.copy, z_grouped[:, c0:c1, :], z_rows[k][:])

        for t in range(2):
            fetch(at_n1, n1_t, t, 0, W)
            fetch(at_n2, n2_t, t, 0, W)
        for k, (c0, c1) in enumerate(Z_CHUNKS):
            if k < 2:
                fetch(at_n1, n1_t, 2, *halves[k])
            if k == 1:
                take_min(0)
            if k < 2:
                fetch(at_n2, n2_t, 2, *halves[k])
            fetch(at_n1, n1_t, 3, c0, c1)
            if k == 2:
                take_min(1)
            fetch(at_n2, n2_t, 3, c0, c1)
            nc.vector.tensor_tensor(
                larger[k][:], at_n1[:, :, c0:c1], y_bf[:, c0 // HALF, :, c0 % HALF : c0 % HALF + c1 - c0], ALU.max
            )
        take_min(2)
        quantize(w1_codes_lo[:], w1_scales[:, :HALF], w1_grouped[0][:])
        for k, (c0, c1) in enumerate(Z_CHUNKS):
            quantize(z_codes[:, c0:c1], z_scales[:, c0:c1], z_grouped[:, c0:c1, :])

        h_win = [sb.tile([P, W], F32, name="h_win%d" % t) for t in range(PACK)]
        h0_copy = sb.tile([P, HALF], F32, name="h0_copy")
        l_codes, l_scales = w1_codes_lo[:, :P], w1_scales[:, :P]
        acc_lo = ps.tile([P, W], F32, name="acc_lo", tag="bank0")
        acc_hi = ps.tile([P, W], F32, name="acc_hi", tag="bank4")
        product(acc_lo[:, :HALF], l_codes, l_scales, z_codes[:, :HALF], z_scales[:, :HALF])
        for c0, c1 in Z_CHUNKS[1:]:
            product(acc_hi[:, c0 - HALF : c1 - HALF], l_codes, l_scales, z_codes[:, c0:c1], z_scales[:, c0:c1])
        nc.scalar.copy(h_win[0][:, :HALF], acc_lo[:, :HALF])
        nc.scalar.copy(h0_copy[:], acc_lo[:, :HALF])
        for u, (c0, c1) in enumerate(halves):
            acc = ps.tile([P, W], F32, name="acc_h1%d" % u, tag=("bank1", "bank5")[u])
            product(acc[:, :HALF], w1_codes_lo[:, P:], w1_scales[:, P:HALF], z_codes[:, c0:c1], z_scales[:, c0:c1])
            nc.scalar.copy(h_win[1][:, c0:c1], acc[:, :HALF])
        w1_codes_hi = sb.tile([P, HALF], U32, name="w1_codes_hi", tag="hold_z0", align_bytes=64)
        quantize(w1_codes_hi[:], w1_scales[:, HALF:], w1_grouped[1][:])
        nc.vector.tensor_copy(h_win[0][:, HALF:], acc_hi[:, :HALF])

        out_rows = out.rearrange("(b t e) n -> t b e n", t=PACK, e=8)
        gate = sb.tile([P, PACK, W], F32, name="gate")
        term_a = sb.tile([P, PACK, W], F32, name="term_a")
        term_b = sb.tile([P, PACK, W], F32, name="term_b")
        result = sb.tile([P, PACK, W], F32, name="result")

        def h_rows(t):
            acc = ps.tile([P, W], F32, name="acc_h%d" % t, tag="bank%d" % t)
            product(acc[:], w1_codes_hi[:, t % 2 * P : (t % 2 + 1) * P], w1_scales[:, t * P : (t + 1) * P], z_codes[:], z_scales[:])
            nc.scalar.copy(h_win[t][:], acc[:])

        def sigmoid_at_n3(t, c0, c1):
            nc.scalar.activation(gate[:, t, c0:c1], h_win[t][:].indirect(entries(n3_t, c0, c1)), ACT.Sigmoid)

        def gated_at_n4(t, c0, c1):
            nc.vector.tensor_tensor(
                term_a[:, t, c0:c1], h_win[t][:].indirect(entries(n4_t, c0, c1)), gate[:, t, c0:c1], ALU.mult
            )

        def gated_in_place(t, c0, c1):
            nc.vector.scalar_tensor_tensor(
                term_b[:, t, c0:c1], gate[:, t, c0:c1], 1.0, h_win[t][:, c0:c1], ALU.subtract, ALU.mult
            )

        def store(t, c0, c1):
            queue = nc.scalar if (t, c1) == (PACK - 1, W) else nc.sync
            queue.dma_start(out_rows[t][:, :, c0:c1], result[:, t, c0:c1])

        def finish(t, c0, c1):
            nc.vector.tensor_tensor(result[:, t, c0:c1], term_a[:, t, c0:c1], term_b[:, t, c0:c1], ALU.subtract)
            store(t, c0, c1)

        lo, hi = halves
        sigmoid_at_n3(0, *hi)
        sigmoid_at_n3(0, *lo)
        nc.vector.tensor_tensor(term_a[:, 0, :HALF], h_win[0][:].indirect(entries(n4_t, *lo)), h0_copy[:], ALU.subtract)
        gated_at_n4(0, *hi)
        nc.vector.tensor_tensor(term_b[:, 0, :HALF], term_a[:, 0, :HALF], gate[:, 0, :HALF], ALU.mult)
        gated_in_place(0, *hi)
        nc.vector.tensor_tensor(result[:, 0, :HALF], term_b[:, 0, :HALF], h0_copy[:], ALU.add)
        store(0, *lo)
        finish(0, *hi)

        for t in range(1, PACK):
            sigmoid_at_n3(t, *lo)
            if t < 3:
                h_rows(t + 1)
            sigmoid_at_n3(t, *hi)
            gated_at_n4(t, *lo)
            if t == 3:
                gated_in_place(3, 0, W)
            if t > 1:
                finish(t - 1, 0, W)
            if t < 3:
                gated_at_n4(t, *hi)
                gated_in_place(t, 0, W)
        for k in (1, 2):
            gated_at_n4(3, *Z_CHUNKS[k])
            finish(3, *Z_CHUNKS[k - 1])
        finish(3, *Z_CHUNKS[2])
